import numpy as np
import ml_dtypes


def mxq(x, axis, fmt="e4m3"):
    dtype, down = {"e4m3": (ml_dtypes.float8_e4m3fn, 7), "e5m2": (ml_dtypes.float8_e5m2, 14)}[fmt]
    v = np.moveaxis(np.asarray(x, np.float32).astype(ml_dtypes.bfloat16).astype(np.float64), axis, -1)
    blocks = v.reshape(v.shape[:-1] + (-1, 32))
    amax = np.abs(blocks).max(-1, keepdims=True)
    byte = np.maximum(np.where(amax > 0, np.frexp(amax)[1] - 1 + 127, 0) - down, 1)
    scale = np.exp2(byte - 127.0)
    codes = (blocks / scale).astype(np.float32).astype(dtype).astype(np.float64)
    return np.moveaxis((codes * scale).reshape(v.shape), -1, axis)


WIDE = False


def mx_kscale(k):
    if not WIDE:
        return np.ones(k)
    levels = np.array([10, -10, 5, -5, 0])
    if k % 512:
        return np.exp2(np.random.permutation(np.resize(levels, k // 32))).repeat(32)
    a = np.empty((k // 512, 16))
    for p in range(k // 512):
        a[p, :8] = np.random.permutation(np.resize(levels, 8))
        for g in range(8):
            far = levels[np.abs(levels - a[p, g]) >= 10]
            a[p, g + 8] = far[np.random.randint(len(far))]
    return np.exp2(a.ravel()).repeat(32)


BF16 = ml_dtypes.bfloat16


def bf(x):
    return np.asarray(x, np.float32).astype(BF16)


def f64(x):
    return np.asarray(x).astype(np.float64)

def planes(Y):
    n, m = Y.shape
    b = f64(bf(Y)).reshape(n // 32, 32, m)
    amax = np.abs(b).max(1)
    byte = np.clip(np.where(amax > 0, np.frexp(amax)[1] - 1 + 127 - 7, 1), 1, 254)
    codes = (b * np.exp2(127.0 - byte)[:, None, :]).reshape(n, m).astype(np.float32).astype(ml_dtypes.float8_e4m3fn).view(np.uint8)
    words = codes.reshape(n // 512, 128, 4, m).transpose(0, 1, 3, 2)
    return np.ascontiguousarray(words), np.ascontiguousarray(byte.astype(np.uint8).reshape(n // 512, 16, m))


T, H, C, E, N = 512, 4, 512, 4, 1024
HC = H * C


def erf(v):
    flat = v.reshape(-1)
    res = np.empty(flat.shape)
    step = 16384
    for i in range(0, flat.size, step):
        c = np.clip(flat[i:i + step], -6.0, 6.0)
        sq = c * c
        q = 2.0 * sq
        tot = np.ones(c.shape)
        for n in range(150, 0, -1):
            tot *= q
            tot /= 2.0 * n + 1.0
            tot += 1.0
        val = 2.0 / np.sqrt(np.pi) * np.exp(-sq) * c * tot
        res[i:i + step] = np.where(np.abs(c) >= 6.0, np.sign(c), val)
    return res.reshape(v.shape)


def exact_gelu(z):
    return 0.5 * z * (1.0 + erf(z / np.sqrt(2.0)))


def softmax(v):
    e = np.exp(v - v.max(-1, keepdims=True))
    return e / e.sum(-1, keepdims=True)


def setup_inputs():
    a, t = mx_kscale(C), mx_kscale(HC)
    return {"x": bf(np.random.standard_normal((T, H, C)) * a),
            "wr": bf(np.random.standard_normal((C, E)) / np.sqrt(C) / a[:, None]),
            "w": bf(np.random.standard_normal((E, C, C)) / np.sqrt(C) / a[:, None]),
            "be": bf(np.random.standard_normal((E, C)) * 0.3),
            "s": bf(np.random.standard_normal((H, C)) * t.reshape(H, C)),
            "wm": bf(np.random.standard_normal((H, C, N)) / np.sqrt(HC) / t.reshape(H, C)[:, :, None])}


def core(x, wr, w, be, s, wm):
    x, wr, w, be, s, wm = f64(x), f64(wr), f64(w), f64(be), f64(s), f64(wm)
    xq = mxq(x.reshape(T * H, C), 1, "e4m3")
    p = xq @ mxq(w, 1, "e4m3")
    p = p.reshape(E, T, H, C).transpose(1, 2, 0, 3) + be
    g = softmax(np.sum(x[..., None, :] * wr.T, axis=-1))
    m = np.sum(g[..., None] * exact_gelu(p), axis=2)
    r = m * s
    return mxq(r.reshape(T, HC), 1, "e4m3") @ mxq(wm.reshape(HC, N), 0, "e4m3")


def reference(x, wr, w, be, s, wm):
    R_out = core(x, wr, w, be, s, wm)
    words, scales = planes(R_out)
    return R_out, words, scales

from contextlib import ExitStack

import concourse.mybir as mybir
from concourse.masks import make_identity

T, H, C, E, N = 512, 4, 512, 4, 1024
FLOPS = 2 * T * H * C * E * C + 2 * T * H * C * E + 2 * T * H * C * N

F32 = mybir.dt.float32
BF16 = mybir.dt.bfloat16
U32 = mybir.dt.uint32
I32 = mybir.dt.int32
U8 = mybir.dt.uint8
FP8X4 = mybir.dt.float8_e4m3fn_x4
ALU = mybir.AluOpType
ACT = mybir.ActivationFunctionType
AX = mybir.AxisListType

P = 128
PACK = 4
BANK = 512
BANKS = 8
HALVES = N // BANK
STEPS = PACK * E
OUT_CHUNK = 256


def tile_multiheadsubtokenmoemerge_x1_kernel(tc, x, wr, w, be, s, wm, out_0, out_1, out_2):
    nc = tc.nc
    with ExitStack() as ctx:
        keep = ctx.enter_context(tc.tile_pool(name="keep", bufs=1))
        work = ctx.enter_context(tc.tile_pool(name="work", bufs=2))
        psum = ctx.enter_context(tc.psum_pool(name="psum", bufs=1))
        ctx.enter_context(tc.manual_schedule())

        used = []

        def bank():
            tag = "bank%d" % (len(used) % BANKS)
            used.append(tag)
            return psum.tile([P, BANK], F32, name=tag, tag=tag)

        def quantize(codes, scales, values):
            nc.vector.quantize_mx(out=codes.bitcast(FP8X4), scales=scales, in_=values)

        x_rows = x.rearrange("(p t) h c -> p t (h c)", t=PACK)
        x_raw = [keep.tile([P, H * C], BF16, name="x_raw%d" % t) for t in range(PACK)]
        w_raw = [keep.tile([P, PACK, C], BF16, name="w_raw%d" % e) for e in range(E)]
        wm_raw = [keep.tile([P, PACK, N], BF16, name="wm_raw%d" % h) for h in range(H)]

        def load_x(t, cols):
            nc.sync.dma_start(out=x_raw[t][:, cols], in_=x_rows[:, t, cols])

        def load_w(e):
            nc.sync.dma_start(out=w_raw[e][:], in_=w[e].rearrange("(p j) d -> p j d", j=PACK))

        def load_wm(h):
            nc.sync.dma_start(out=wm_raw[h][:], in_=wm[h].rearrange("(p j) n -> p j n", j=PACK))

        be_rows = keep.tile([E * PACK, P], BF16, name="be_rows")
        s_sb = keep.tile([P, H, PACK], BF16, name="s_sb")
        wr_sb = keep.tile([P, PACK, E], BF16, name="wr_sb")
        load_x(0, slice(0, 2 * C))
        load_x(0, slice(2 * C, 4 * C))
        load_w(0)
        nc.scalar.dma_start(out=be_rows[:], in_=be.rearrange("e (b p) -> (e b) p", p=P))
        nc.scalar.dma_start(out=wr_sb[:], in_=wr.rearrange("(p j) e -> p j e", j=PACK))
        nc.scalar.dma_start(out=s_sb[:], in_=s.rearrange("h (p j) -> p h j", j=PACK))
        load_w(1)
        load_w(2)
        load_x(1, slice(0, H * C))
        load_w(3)
        load_wm(0)
        load_wm(1)
        load_x(2, slice(0, H * C))
        load_wm(2)
        load_wm(3)
        load_x(3, slice(0, H * C))

        ident = keep.tile([P, P], F32, name="ident")
        make_identity(nc, ident[:])
        be_pad = keep.tile([P, P], F32, name="be_pad")
        nc.vector.memset(be_pad[:], 0.0)
        warm = keep.tile([P, 1], F32, name="warm")
        nc.scalar.activation(out=warm[:], in_=be_pad[:, 0:1], func=ACT.Gelu)
        bias = keep.tile([P, E * PACK], F32, name="bias")

        w_codes = keep.tile([P, E, C], U32, name="w_codes", align_bytes=64)
        w_scales = keep.tile([P, E, C], U8, name="w_scales", align_bytes=64)
        wm_codes = keep.tile([P, H, N], U32, name="wm_codes", align_bytes=64)
        wm_scales = keep.tile([P, H, N], U8, name="wm_scales", align_bytes=64)
        r_codes = [keep.tile([P, H * P], U32, name="r_codes%d" % t, align_bytes=64) for t in range(PACK)]
        r_scales = [keep.tile([P, H * P], U8, name="r_scales%d" % t, align_bytes=64) for t in range(PACK)]
        out_f32 = keep.tile([P, PACK, N], F32, name="out_f32")
        out_rows = out_0.rearrange("(p t) n -> p t n", t=PACK)

        xg, x_codes, x_scales, gates, acc, r_bf, y = {}, {}, {}, {}, {}, {}, {}
        logit = {}
        grouped = {}

        def group_w(e):
            tag = "pool_grouped" if e == E - 1 else "w_grouped"
            g = work.tile([P, BANK, PACK], BF16, name=tag, tag=tag, bufs=1 if e == E - 1 else 2, align_bytes=64)
            nc.vector.tensor_copy(out=g[:], in_=w_raw[e][:].rearrange("p j d -> p d j"))
            grouped["w", e] = g

        def quant_w(e):
            quantize(w_codes[:, e, :], w_scales[:, e, :], grouped["w", e][:].rearrange("p d j -> p (d j)"))

        def group_wm(c):
            half, h = divmod(c, H)
            g = work.tile([P, BANK, PACK], BF16, name="pool_grouped", tag="pool_grouped", bufs=1, align_bytes=64)
            src = wm_raw[h][:, :, half * BANK : (half + 1) * BANK].rearrange("p j n -> p n j")
            nc.gpsimd.tensor_scalar(out=g[:], in0=src, scalar1=1.0, scalar2=0.0, op0=ALU.mult, op1=ALU.add)
            grouped["wm", c] = g

        def quant_wm(c):
            half, h = divmod(c, H)
            cols = slice(half * BANK, (half + 1) * BANK)
            quantize(wm_codes[:, h, cols], wm_scales[:, h, cols], grouped["wm", c][:].rearrange("p n j -> p (n j)"))

        def turn_x(t):
            xg[t] = work.tile([P, H, P, PACK], BF16, name="xg", tag="xg", align_bytes=64)
            words = x_raw[t][:].bitcast(F32)
            dst = xg[t][:].rearrange("p h q j -> p (h q j)").bitcast(F32).rearrange("p (h q u) -> p h q u", h=H, u=2)
            for pair in range(H // 2):
                b = bank()
                for hh in range(2):
                    h = 2 * pair + hh
                    for u in range(2):
                        col = (2 * hh + u) * P
                        nc.tensor.transpose(b[:, col : col + P], words[:, 256 * h + u : 256 * (h + 1) : 2], ident[:])
                nc.scalar.copy(
                    out=dst[:, 2 * pair : 2 * pair + 2], in_=b[:].rearrange("p (h u q) -> p h q u", h=2, u=2)
                )

        def quant_x(t):
            x_codes[t] = work.tile([P, H * P], U32, name="x_codes", tag="x_codes", align_bytes=64)
            x_scales[t] = work.tile([P, H * P], U8, name="x_scales", tag="x_scales", align_bytes=64)
            quantize(x_codes[t][:], x_scales[t][:], xg[t][:].rearrange("p h q j -> p (h q j)"))

        def route(t):
            b = bank()
            for h in range(H):
                for j in range(PACK):
                    nc.tensor.matmul(
                        b[:, h * E : (h + 1) * E], lhsT=xg[t][:, h, :, j], rhs=wr_sb[:, j, :],
                        start=(j == 0), stop=(j == PACK - 1),
                    )
            logits = b[:, : H * E].rearrange("q (h e) -> q h e", e=E)
            top = work.tile([P, H], F32, name="top", tag="top")
            nc.vector.tensor_reduce(out=top[:], in_=logits, axis=AX.X, op=ALU.max)
            diff = work.tile([P, H, E], F32, name="diff", tag="diff")
            nc.vector.tensor_tensor(
                out=diff[:], in0=logits, in1=top[:].unsqueeze(2).to_broadcast([P, H, E]), op=ALU.subtract
            )
            logit[t] = diff

        def route_tanh(t):
            th = work.tile([P, H, E], F32, name="th", tag="th")
            nc.scalar.activation(out=th[:], in_=logit[t][:], func=ACT.Tanh, scale=0.5)
            den = work.tile([P, H, E], F32, name="den", tag="den")
            nc.scalar.activation(out=den[:], in_=th[:], func=ACT.Copy, scale=-1.0, bias=1.0)
            logit[t] = (th, den)

        def route_gates(t):
            th, den = logit[t]
            rden = work.tile([P, H, E], F32, name="rden", tag="rden")
            nc.vector.reciprocal(out=rden[:], in_=den[:])
            ex = work.tile([P, H, E], F32, name="ex", tag="ex")
            nc.vector.scalar_tensor_tensor(out=ex[:], in0=th[:], scalar=1.0, in1=rden[:], op0=ALU.add, op1=ALU.mult)
            tot = work.tile([P, H], F32, name="tot", tag="tot")
            nc.vector.tensor_reduce(out=tot[:], in_=ex[:], axis=AX.X, op=ALU.add)
            rtot = work.tile([P, H], F32, name="rtot", tag="rtot")
            nc.vector.reciprocal(out=rtot[:], in_=tot[:])
            gates[t] = work.tile([P, H, E], F32, name="gates", tag="gates")
            nc.vector.tensor_tensor(
                out=gates[t][:], in0=ex[:], in1=rtot[:].unsqueeze(2).to_broadcast([P, H, E]), op=ALU.mult
            )

        def experts(k):
            t, e = divmod(k, E)
            y[k] = work.tile([P, PACK, H * P], F32, name="y", tag="y", bufs=3)
            for blk in range(PACK):
                b = bank()
                cols = slice(blk * P, (blk + 1) * P)
                nc.tensor.matmul_mx(
                    out=b[:], lhsT=w_codes[:, e, cols].bitcast(FP8X4), lhsT_scale=w_scales[:, e, cols],
                    rhs=x_codes[t][:].bitcast(FP8X4), rhs_scale=x_scales[t][:], start=True, stop=True,
                )
                col = e * PACK + blk
                nc.scalar.activation(out=y[k][:, blk, :], in_=b[:], func=ACT.Gelu, bias=bias[:, col : col + 1])

        def turn_y(k, h):
            b = bank()
            for blk in range(PACK):
                nc.tensor.transpose(b[:, blk * P : (blk + 1) * P], y[k][:, blk, h * P : (h + 1) * P], ident[:])
            return b

        def gate(k, h, b):
            t, e = divmod(k, E)
            src = b[:].rearrange("q (m j) -> q j m", j=PACK)
            g = gates[t][:, h, e : e + 1]
            if e == 0:
                acc[t, h] = work.tile([P, PACK, P], F32, name="acc%d" % h, tag="acc%d" % h)
                nc.scalar.activation(out=acc[t, h][:], in_=src, func=ACT.Copy, scale=g)
            else:
                a = acc[t, h][:]
                nc.vector.scalar_tensor_tensor(out=a, in0=src, scalar=g, in1=a, op0=ALU.mult, op1=ALU.add)

        def turn_back(t, h):
            if h == 0:
                r_bf[t] = work.tile([P, H, P, PACK], BF16, name="r_bf", tag="r_bf", align_bytes=64)
            b = bank()
            for j in range(PACK):
                nc.tensor.transpose(b[:, j * P : (j + 1) * P], acc[t, h][:, j, :], ident[:])
            nc.vector.tensor_tensor(
                out=r_bf[t][:, h], in0=b[:].rearrange("p (j q) -> p q j", j=PACK),
                in1=s_sb[:, h : h + 1, :].to_broadcast([P, P, PACK]), op=ALU.mult,
            )

        def quant_r(t, heads):
            cols = slice(heads.start * P, heads.stop * P)
            quantize(r_codes[t][:, cols], r_scales[t][:, cols], r_bf[t][:, heads].rearrange("p h q j -> p (h q j)"))

        def merge_pass(b, t, half, h):
            cols = slice(half * BANK, (half + 1) * BANK)
            toks = slice(h * P, (h + 1) * P)
            nc.tensor.matmul_mx(
                out=b[:], lhsT=r_codes[t][:, toks].bitcast(FP8X4), lhsT_scale=r_scales[t][:, toks],
                rhs=wm_codes[:, h, cols].bitcast(FP8X4), rhs_scale=wm_scales[:, h, cols],
                start=(h == 0), stop=(h == H - 1),
            )

        def store_rows(t, half):
            cols = slice(half * BANK, (half + 1) * BANK)
            nc.sync.dma_start(out=out_rows[:, t, cols], in_=out_f32[:, t, cols])

        def merge(t, half):
            b = bank()
            for h in range(H):
                merge_pass(b, t, half, h)
            nc.scalar.copy(out=out_f32[:, t, half * BANK : (half + 1) * BANK], in_=b[:])
            store_rows(t, half)

        nc.vector.tensor_copy(out=be_pad[: E * PACK, :], in_=be_rows[:])
        turn_x(0)
        b = bank()
        nc.tensor.transpose(b[:, :P], be_pad[:], ident[:])
        group_w(0)
        nc.vector.tensor_copy(out=bias[:], in_=b[:, : E * PACK])
        quant_w(0)
        quant_x(0)
        group_w(1)

        merges = {7: [(0, 0)], 11: [(0, 1)], 12: [(1, 0)], 13: [(1, 1)], 14: [(2, 0)], 15: [(2, 1)]}
        for k in range(STEPS):
            t, e = divmod(k, E)
            experts(k)
            for job in merges.get(k, []):
                merge(*job)
            if k == 0:
                quant_w(1)
                route(0)
                group_w(2)
            if e == 0:
                route_tanh(t)
            if k == 0:
                quant_w(2)
            if e == 1:
                route_gates(t)
            if k == 1:
                group_w(3)
            if e == 2 and 1 <= t < PACK - 1:
                quant_r(t - 1, slice(0, H))
            if e == 3 and t + 1 < PACK:
                quant_x(t + 1)
            if k == 2:
                quant_w(3)
                group_wm(0)
            if 3 <= k < 3 + H * HALVES:
                quant_wm(k - 3)
                if k - 2 < H * HALVES:
                    group_wm(k - 2)
            if e == 1 and t >= 1:
                for h in range(H):
                    turn_back(t - 1, h)
                if t == PACK - 1:
                    quant_r(t - 1, slice(0, H))
            if k >= 1:
                for h in range(H):
                    gate(k - 1, h, turn_y(k - 1, h))
            if e == 2 and t + 1 < PACK:
                turn_x(t + 1)
            if e == 3 and t + 1 < PACK:
                route(t + 1)

        k, t = STEPS - 1, PACK - 1
        for h in range(H - 1):
            gate(k, h, turn_y(k, h))
        last = turn_y(k, H - 1)
        turn_back(t, 0)
        gate(k, H - 1, last)
        for h in range(1, H):
            turn_back(t, h)
            quant_r(t, slice(h - 1, h))
        quant_r(t, slice(H - 1, H))
        ends = [bank() for half in range(HALVES)]
        for h in range(H):
            for half in range(HALVES):
                merge_pass(ends[half], t, half, h)
        nc.scalar.copy(out=out_f32[:, t, :BANK], in_=ends[0][:])
        nc.vector.tensor_copy(out=out_f32[:, t, BANK:], in_=ends[1][:])
        for half in range(HALVES):
            store_rows(t, half)

        out_codes = keep.tile([P, N], U32, name="out_codes", align_bytes=64)
        out_scales = keep.tile([P, N], U8, name="out_scales", align_bytes=64)
        words = out_1[0].rearrange("p m t -> p (m t)").bitcast(I32)
        chunks = [slice(c, c + OUT_CHUNK) for c in range(0, N, OUT_CHUNK)]
        out_bf = [keep.tile([P, OUT_CHUNK, PACK], BF16, name="out_bf%d" % c, align_bytes=64) for c in range(len(chunks))]
        for c, cols in enumerate(chunks):
            src = out_f32[:, :, cols].rearrange("p t n -> p n t")
            if c % 2 == 0:
                nc.vector.tensor_copy(out=out_bf[c][:], in_=src)
            else:
                nc.scalar.copy(out=out_bf[c][:], in_=src)
        for c in (0, 2, 1, 3):
            cols = chunks[c]
            quantize(out_codes[:, cols], out_scales[:, cols], out_bf[c][:].rearrange("p n t -> p (n t)"))
            nc.sync.dma_start(out=words[:, cols], in_=out_codes[:, cols].bitcast(I32))
        for q in range(4):
            eng = nc.sync if q % 2 == 0 else nc.scalar
            eng.dma_start(
                out=out_2[0, 4 * q : 4 * q + 4, :].bitcast(I32), in_=out_scales[32 * q : 32 * q + 4, :].bitcast(I32)
            )
